import numpy as np
import ml_dtypes


def mxq(x, axis, fmt="e4m3"):
    dtype, down = {"e4m3": (ml_dtypes.float8_e4m3fn, 7), "e5m2": (ml_dtypes.float8_e5m2, 14)}[fmt]
    v = np.moveaxis(np.asarray(x, np.float32).astype(ml_dtypes.bfloat16).astype(np.float64), axis, -1)
    blocks = v.reshape(v.shape[:-1] + (-1, 32))
    amax = np.abs(blocks).max(-1, keepdims=True)
    byte = np.maximum(np.where(amax > 0, np.frexp(amax)[1] - 1 + 127, 0) - down, 1)
    scale = np.exp2(byte - 127.0)
    codes = (blocks / scale).astype(np.float32).astype(dtype).astype(np.float64)
    return np.moveaxis((codes * scale).reshape(v.shape), -1, axis)


WIDE = False


def mx_kscale(k):
    if not WIDE:
        return np.ones(k)
    levels = np.array([10, -10, 5, -5, 0])
    if k % 512:
        return np.exp2(np.random.permutation(np.resize(levels, k // 32))).repeat(32)
    a = np.empty((k // 512, 16))
    for p in range(k // 512):
        a[p, :8] = np.random.permutation(np.resize(levels, 8))
        for g in range(8):
            far = levels[np.abs(levels - a[p, g]) >= 10]
            a[p, g + 8] = far[np.random.randint(len(far))]
    return np.exp2(a.ravel()).repeat(32)


def f64(x):
    return np.asarray(x).astype(np.float64)


def striped(idx):
    return np.tile(np.asarray(idx).reshape(-1, 16).T, (8, 1)).astype(np.uint16)


def unstriped(offs):
    return offs[:16].T.reshape(-1).astype(np.int64)


E2M1 = np.array([0.0, 0.5, 1.0, 1.5, 2.0, 3.0, 4.0, 6.0, -0.0, -0.5, -1.0, -1.5, -2.0, -3.0, -4.0, -6.0])


def pack_weight(w, fmt):
    k, n = w.shape
    w = f64(np.asarray(w, np.float32).astype(ml_dtypes.bfloat16)).reshape(k // 32, 32, n)
    amax = np.abs(w).max(1)
    if fmt == "e4m3":
        byte = np.frexp(amax)[1] - 1 + 127 - 7
    else:
        mant, ex = np.frexp(amax / 6.0)
        byte = np.where(mant > 0.5, ex, ex - 1) + 127
    byte = np.clip(np.where(amax > 0, byte, 1), 1, 254)
    scaled = (w * np.exp2(127.0 - byte)[:, None, :]).reshape(k, n).astype(np.float32)
    by_word = np.ascontiguousarray(scaled.reshape(k // 512, 128, 4, n).transpose(0, 1, 3, 2))
    if fmt == "e4m3":
        words = by_word.astype(ml_dtypes.float8_e4m3fn).view(np.uint8)
    else:
        c = by_word.astype(ml_dtypes.float4_e2m1fn).view(np.uint8) & 0xF
        words = (c[..., 0::2] | (c[..., 1::2] << 4)).reshape(k // 512, 128, 2 * n)
    return np.ascontiguousarray(words), np.ascontiguousarray(byte.astype(np.uint8).reshape(k // 512, 16, n))


def unpack_weight(words, scales, fmt):
    g, _, n = scales.shape
    words = np.ascontiguousarray(words).reshape(g, 128, n, -1)
    if fmt == "e4m3":
        vals = words.view(ml_dtypes.float8_e4m3fn).astype(np.float64)
    else:
        nib = np.empty((g, 128, n, 4), np.uint8)
        nib[..., 0::2] = words & 0xF
        nib[..., 1::2] = words >> 4
        vals = E2M1[nib]
    vals = vals * np.repeat(np.exp2(scales.astype(np.float64) - 127.0), 8, axis=1)[..., None]
    return vals.transpose(0, 1, 3, 2).reshape(g * 512, n)


def bf(x):
    return np.asarray(x, np.float32).astype(ml_dtypes.bfloat16)


def planes(Y):
    r, m = Y.shape
    b = f64(bf(Y)).reshape(r // 32, 32, m)
    amax = np.abs(b).max(1)
    byte = np.clip(np.where(amax > 0, np.frexp(amax)[1] - 1 + 127 - 7, 1), 1, 254)
    codes = (b * np.exp2(127.0 - byte)[:, None, :]).reshape(r, m).astype(np.float32).astype(ml_dtypes.float8_e4m3fn).view(np.uint8)
    words = codes.reshape(r // 512, 128, 4, m).transpose(0, 1, 3, 2)
    return np.ascontiguousarray(words), np.ascontiguousarray(byte.astype(np.uint8).reshape(r // 512, 16, m))


K, T, J, R, N = 512, 2048, 512, 512, 512


def setup_inputs():
    n = np.random.standard_normal
    idx = np.random.permutation(T)[:J]
    fk = mx_kscale(K)
    fr = mx_kscale(R)
    xtp = pack_weight(n((K, T)) / fk[:, None], "e2m1")
    wap = pack_weight(n((K, R)) * 1 / np.sqrt(K) * fk[:, None], "e4m3")
    wbp = pack_weight(n((R, N)) * 1 / np.sqrt(R) / fr[:, None], "e2m1")
    return {
        "xt_words": xtp[0],
        "xt_scales": xtp[1],
        "wa_words": wap[0],
        "wa_scales": wap[1],
        "us": (np.random.uniform(0.5, 2.0, (R, 1)) * fr[:, None]).astype(np.float32),
        "wb_words": wbp[0],
        "wb_scales": wbp[1],
        "rw": (np.random.uniform(0.5, 2.0, (1, J))).astype(np.float32),
        "offs": striped(idx),
    }


def reference(xt_words, xt_scales, wa_words, wa_scales, us, wb_words, wb_scales, rw, offs):
    idx = unstriped(offs)
    xtu = unpack_weight(xt_words, xt_scales, "e2m1")
    wau = unpack_weight(wa_words, wa_scales, "e4m3")
    wbu = unpack_weight(wb_words, wb_scales, "e2m1")
    xtidxg = xtu[:, idx]
    a = wau.T @ xtidxg
    hid = a / (np.mean(np.abs(a), axis=1, keepdims=True) + 0.1) * f64(us)
    hidq = mxq(hid, 0, "e4m3")
    p = wbu.T @ hidq
    y = p * f64(rw)
    words, scales = planes(y)
    return y, words, scales

@@ -1,0 +1,242 @@
+from contextlib import ExitStack
+
+import concourse.mybir as mybir
+
+K, T, J, R, N = 512, 2048, 512, 512, 512
+FLOPS = 2 * K * R * J + 2 * R * N * J
+
+F32 = mybir.dt.float32
+BF16 = mybir.dt.bfloat16
+I32 = mybir.dt.int32
+U32 = mybir.dt.uint32
+U16 = mybir.dt.uint16
+U8 = mybir.dt.uint8
+FP8X4 = mybir.dt.float8_e4m3fn_x4
+FP4X4 = mybir.dt.float4_e2m1fn_x4
+ACT = mybir.ActivationFunctionType
+ALU = mybir.AluOpType
+AX = mybir.AxisListType
+
+P = 128
+PACK = 4
+QUADS = 4
+CHUNK = 128
+CHUNKS = J // CHUNK
+HALF = J // 2
+VECTOR_SUM_CHUNK = 2
+
+
+def load_scale_rows(queue, plane, rows, quads):
+    for q in quads:
+        queue.dma_start(out=plane[32 * q : 32 * q + 4, :].bitcast(I32), in_=rows[4 * q : 4 * q + 4, :].bitcast(I32))
+
+
+def load_scale_quadrants(queue, plane, rows, quads):
+    width = rows.shape[1] // 4
+    for q in quads:
+        four = rows[4 * q : 4 * q + 4, :].bitcast(I32)
+        queue.dma_start(
+            out=plane[32 * q : 32 * q + 32, :].bitcast(I32), in_=four.unsqueeze(0).to_broadcast([8, 4, width])
+        )
+
+
+def tile_list_hidden_evened_pl_kernel(
+    tc, xt_words, xt_scales, wa_words, wa_scales, us, wb_words, wb_scales, rw, offs, out_0, out_1, out_2
+):
+    nc = tc.nc
+    with ExitStack() as ctx:
+        keep = ctx.enter_context(tc.tile_pool(name="keep", bufs=1))
+        shared = ctx.enter_context(tc.tile_pool(name="shared", bufs=1))
+        psum = ctx.enter_context(tc.psum_pool(name="psum", bufs=1))
+
+        offsets = keep.tile([P, J // 16], U16, name="offsets")
+        x_words = keep.tile([P, T], U16, name="x_words", align_bytes=64)
+        x_scales = keep.tile([P, T], U8, name="x_scales", align_bytes=64)
+        wa_raw = keep.tile([P, R], I32, name="wa_raw", tag="wa_raw", align_bytes=64)
+        wa_scale_raw = shared.tile([P, R], U8, name="wa_scale_raw", offset=0)
+
+        nc.vector.memset(x_scales[:].bitcast(I32), 0)
+
+        nc.sync.dma_start(offsets[:], offs)
+        load_scale_quadrants(nc.scalar, wa_scale_raw, wa_scales[0], (1, 2, 3))
+        load_scale_quadrants(nc.sync, wa_scale_raw, wa_scales[0], (0,))
+        nc.sync.dma_start(out=x_words[:].bitcast(I32), in_=xt_words[0].bitcast(I32))
+        nc.sync.dma_start(out=wa_raw[:], in_=wa_words[0].rearrange("p c t -> p (c t)").bitcast(I32))
+        load_scale_rows(nc.scalar, x_scales, xt_scales[0], range(QUADS))
+
+        wa_codes = keep.tile([P, PACK, P], I32, name="wa_codes", align_bytes=64)
+        wa_scale = keep.tile([P, PACK, P], U8, name="wa_scale", align_bytes=64)
+        nc.vector.tensor_copy(out=wa_scale[:], in_=wa_scale_raw[:].rearrange("p (m t) -> p t m", t=PACK))
+
+        us_sb = shared.tile([P, PACK], F32, name="us_sb", offset=0)
+        wb_raw = shared.tile([P, 3 * N], U8, name="wb_raw", offset=64)
+        nc.sync.dma_start(out=us_sb[:], in_=us.rearrange("(p t) o -> p (t o)", t=PACK))
+        load_scale_quadrants(nc.sync, wb_raw[:, 0:N], wb_scales[0], range(QUADS))
+        nc.sync.dma_start(out=wb_raw[:, N : 3 * N].bitcast(I32), in_=wb_words[0].bitcast(I32))
+
+        sums = keep.tile([P, CHUNKS, PACK], F32, name="sums")
+
+        a_banks = []
+        magnitudes = keep.tile([P, CHUNKS, PACK, CHUNK], BF16, name="magnitudes")
+        for h in range(2):
+            cols = offsets[:, h * HALF // 16 : (h + 1) * HALF // 16]
+            g_scales = keep.tile([P, HALF], U8, name=f"g_scales{h}", align_bytes=64)
+            g_words = keep.tile([P, HALF], U16, name=f"g_words{h}", align_bytes=64)
+            nc.vector.tensor_copy(out=g_words[:], in_=x_words[:].indirect(cols))
+            nc.vector.tensor_copy(out=g_scales[:], in_=x_scales[:].indirect(cols))
+            if h == 0:
+                nc.vector.tensor_copy(
+                    out=wa_codes[:].rearrange("p t m -> p m t"), in_=wa_raw[:].rearrange("p (m t) -> p m t", t=PACK)
+                )
+            for u in range(2):
+                c = 2 * h + u
+                bank = psum.tile([P, PACK, CHUNK], F32, name=f"a_bank{c}")
+                js = slice(u * CHUNK, (u + 1) * CHUNK)
+                for t in range(PACK):
+                    nc.tensor.matmul_mx(
+                        out=bank[:, t, :],
+                        lhsT=wa_codes[:, t, :].bitcast(FP8X4),
+                        lhsT_scale=wa_scale[:, t, :],
+                        rhs=g_words[:, js].bitcast(FP4X4),
+                        rhs_scale=g_scales[:, js],
+                        start=True,
+                        stop=True,
+                    )
+                a_banks.append(bank)
+
+        rw_rows = keep.tile([P, J], F32, name="rw_rows", tag="wa_raw", align_bytes=64)
+        nc.sync.dma_start(out=rw_rows[:], in_=rw[0].partition_broadcast(P))
+
+        wb_codes = keep.tile([P, PACK, P], U16, name="wb_codes", align_bytes=64)
+        wb_scale = keep.tile([P, PACK, P], U8, name="wb_scale", align_bytes=64)
+        nc.vector.tensor_copy(out=wb_scale[:], in_=wb_raw[:, 0:N].rearrange("p (m t) -> p t m", t=PACK))
+        nc.vector.tensor_copy(
+            out=wb_codes[:], in_=wb_raw[:, N : 3 * N].bitcast(U16).rearrange("p (m t) -> p t m", t=PACK)
+        )
+
+        inv_us = keep.tile([P, PACK], F32, name="inv_us")
+        nc.vector.reciprocal(out=inv_us[:], in_=us_sb[:])
+        for c in range(CHUNKS):
+            if c == VECTOR_SUM_CHUNK:
+                a_copy = keep.tile([P, PACK, CHUNK], F32, name="a_copy")
+                nc.vector.tensor_copy(out=a_copy[:], in_=a_banks[c][:])
+                nc.vector.tensor_reduce(
+                    out=sums[:, c, :], in_=a_copy[:], axis=AX.X, op=ALU.add, apply_absolute_value=True
+                )
+            else:
+                for t in range(PACK):
+                    nc.scalar.activation(
+                        out=magnitudes[:, c, t, :], in_=a_banks[c][:, t, :], func=ACT.Abs, accum_out=sums[:, c, t : t + 1]
+                    )
+
+        early = keep.tile([P, PACK], F32, name="early")
+        early2 = keep.tile([P, PACK], F32, name="early2")
+        denom = keep.tile([P, PACK], F32, name="denom")
+        factor = keep.tile([P, PACK], F32, name="factor")
+        slope = keep.tile([P, PACK], F32, name="slope")
+        nc.vector.tensor_scalar(out=slope[:], in0=inv_us[:], scalar1=1.0 / J, scalar2=None, op0=ALU.mult)
+        nc.vector.scalar_tensor_tensor(
+            out=early[:], in0=sums[:, 0, :], scalar=0.1 * J, in1=sums[:, 1, :], op0=ALU.add, op1=ALU.add
+        )
+        nc.vector.tensor_tensor(out=early2[:], in0=early[:], in1=sums[:, 2, :], op=ALU.add)
+        for t in range(PACK):
+            nc.vector.tensor_scalar(
+                out=denom[:, t : t + 1],
+                in0=sums[:, 3, t : t + 1],
+                scalar1=early2[:, t : t + 1],
+                scalar2=slope[:, t : t + 1],
+                op0=ALU.add,
+                op1=ALU.mult,
+            )
+        nc.vector.reciprocal(out=factor[:], in_=denom[:])
+
+        hid = [keep.tile([P, CHUNK, PACK], BF16, name=f"hid{c}", align_bytes=64) for c in range(CHUNKS)]
+        h_codes = [keep.tile([P, CHUNK], U32, name=f"h_codes{c}", align_bytes=64) for c in range(CHUNKS)]
+        h_scale = [keep.tile([P, CHUNK], U8, name=f"h_scale{c}", align_bytes=64) for c in range(CHUNKS)]
+        y = [keep.tile([P, PACK, CHUNK], F32, name=f"y{c}", align_bytes=64) for c in range(CHUNKS)]
+        y16 = [keep.tile([P, CHUNK, PACK], BF16, name=f"y16_{c}", align_bytes=64) for c in range(CHUNKS)]
+        y_codes = keep.tile([P, J], U32, name="y_codes", align_bytes=64)
+        y_scale = keep.tile([P, J], U8, name="y_scale", align_bytes=64)
+        p_banks = {}
+        y_rows = out_0.rearrange("(p t) j -> p t j", t=PACK)
+
+        def scale_hid(c):
+            nc.vector.tensor_tensor(
+                out=hid[c][:],
+                in0=a_banks[c][:].rearrange("p t j -> p j t"),
+                in1=factor[:].unsqueeze(1).to_broadcast([P, CHUNK, PACK]),
+                op=ALU.mult,
+            )
+
+        def scale_hid_on_scalar(c):
+            rows = keep.tile([P, PACK, CHUNK], BF16, name=f"hid_rows{c}")
+            for t in range(PACK):
+                nc.scalar.activation(
+                    out=rows[:, t, :], in_=a_banks[c][:, t, :], func=ACT.Copy, scale=factor[:, t : t + 1]
+                )
+            nc.scalar.copy(
+                out=hid[c][:].rearrange("p (g i) t -> p g t i", i=4),
+                in_=rows[:].rearrange("p t (g i) -> p g t i", i=4),
+            )
+
+        def second_product(c):
+            nc.vector.quantize_mx(
+                out=h_codes[c][:].bitcast(FP8X4), scales=h_scale[c][:], in_=hid[c][:].rearrange("p j t -> p (j t)")
+            )
+            bank = psum.tile([P, PACK, CHUNK], F32, name=f"p_bank{c}", tag=f"p_bank{c}")
+            for t in range(PACK):
+                nc.tensor.matmul_mx(
+                    out=bank[:, t, :],
+                    lhsT=wb_codes[:, t, :].bitcast(FP4X4),
+                    lhsT_scale=wb_scale[:, t, :],
+                    rhs=h_codes[c][:].bitcast(FP8X4),
+                    rhs_scale=h_scale[c][:],
+                    start=True,
+                    stop=True,
+                )
+            p_banks[c] = bank
+
+        def weigh(c):
+            js = slice(c * CHUNK, (c + 1) * CHUNK)
+            nc.vector.tensor_tensor(
+                out=y[c][:],
+                in0=p_banks[c][:],
+                in1=rw_rows[:, js].unsqueeze(1).to_broadcast([P, PACK, CHUNK]),
+                op=ALU.mult,
+            )
+            nc.sync.dma_start(out=y_rows[:, :, js], in_=y[c][:])
+            nc.scalar.copy(
+                out=y16[c][:].rearrange("p (g i) t -> p g t i", i=4),
+                in_=y[c][:].rearrange("p t (g i) -> p g t i", i=4),
+            )
+
+        def planes(c):
+            js = slice(c * CHUNK, (c + 1) * CHUNK)
+            nc.vector.quantize_mx(
+                out=y_codes[:, js].bitcast(FP8X4), scales=y_scale[:, js], in_=y16[c][:].rearrange("p j t -> p (j t)")
+            )
+
+        scale_hid(0)
+        scale_hid(1)
+        scale_hid_on_scalar(2)
+        scale_hid_on_scalar(3)
+        second_product(0)
+        second_product(1)
+        second_product(2)
+        weigh(0)
+        weigh(1)
+        second_product(3)
+        weigh(2)
+        planes(0)
+        planes(1)
+        weigh(3)
+        planes(2)
+        words_out = out_1[0].rearrange("p c t -> p (c t)").bitcast(I32)
+        nc.sync.dma_start(out=words_out[:, 0 : 3 * CHUNK], in_=y_codes[:, 0 : 3 * CHUNK].bitcast(I32))
+        planes(3)
+        nc.sync.dma_start(out=words_out[:, 3 * CHUNK : J], in_=y_codes[:, 3 * CHUNK : J].bitcast(I32))
+        for q in range(QUADS):
+            queue = nc.scalar if q % 2 == 0 else nc.sync
+            queue.dma_start(
+                out=out_2[0, 4 * q : 4 * q + 4, :].bitcast(I32), in_=y_scale[32 * q : 32 * q + 4, :].bitcast(I32)
+            )

@@ -23,7 +23,7 @@ QUADS = 4
 CHUNK = 128
 CHUNKS = J // CHUNK
 HALF = J // 2
-VECTOR_SUM_CHUNK = 2
+VECTOR_SUM_CHUNK = 1
 
 
 def load_scale_rows(queue, plane, rows, quads):
@@ -52,27 +52,28 @@ def tile_list_hidden_evened_pl_kernel(
         offsets = keep.tile([P, J // 16], U16, name="offsets")
         x_words = keep.tile([P, T], U16, name="x_words", align_bytes=64)
         x_scales = keep.tile([P, T], U8, name="x_scales", align_bytes=64)
-        wa_raw = keep.tile([P, R], I32, name="wa_raw", tag="wa_raw", align_bytes=64)
-        wa_scale_raw = shared.tile([P, R], U8, name="wa_scale_raw", offset=0)
+        wa_raw = keep.tile([P, R], I32, name="wa_raw", align_bytes=64)
+        wa_scale_raw = shared.tile([P, R], U8, name="wa_scale_raw", offset=2 * HALF, align_bytes=64)
+        wb_raw = keep.tile([P, N], U16, name="wb_raw", align_bytes=64)
+        wb_scale_raw = keep.tile([P, N], U8, name="wb_scale_raw", align_bytes=64)
+        us_sb = keep.tile([P, PACK], F32, name="us_sb")
+        rw_rows = keep.tile([P, J], F32, name="rw_rows")
 
         nc.vector.memset(x_scales[:].bitcast(I32), 0)
 
         nc.sync.dma_start(offsets[:], offs)
-        load_scale_quadrants(nc.scalar, wa_scale_raw, wa_scales[0], (1, 2, 3))
+        load_scale_rows(nc.scalar, x_scales, xt_scales[0], range(QUADS))
         load_scale_quadrants(nc.sync, wa_scale_raw, wa_scales[0], (0,))
         nc.sync.dma_start(out=x_words[:].bitcast(I32), in_=xt_words[0].bitcast(I32))
         nc.sync.dma_start(out=wa_raw[:], in_=wa_words[0].rearrange("p c t -> p (c t)").bitcast(I32))
-        load_scale_rows(nc.scalar, x_scales, xt_scales[0], range(QUADS))
+        load_scale_quadrants(nc.sync, wa_scale_raw, wa_scales[0], (1, 2, 3))
+        nc.sync.dma_start(out=us_sb[:], in_=us.rearrange("(p t) o -> p (t o)", t=PACK))
+        load_scale_quadrants(nc.sync, wb_scale_raw, wb_scales[0], range(QUADS))
+        nc.sync.dma_start(out=wb_raw[:].bitcast(I32), in_=wb_words[0].bitcast(I32))
+        nc.sync.dma_start(out=rw_rows[:], in_=rw[0].partition_broadcast(P))
 
         wa_codes = keep.tile([P, PACK, P], I32, name="wa_codes", align_bytes=64)
         wa_scale = keep.tile([P, PACK, P], U8, name="wa_scale", align_bytes=64)
-        nc.vector.tensor_copy(out=wa_scale[:], in_=wa_scale_raw[:].rearrange("p (m t) -> p t m", t=PACK))
-
-        us_sb = shared.tile([P, PACK], F32, name="us_sb", offset=0)
-        wb_raw = shared.tile([P, 3 * N], U8, name="wb_raw", offset=64)
-        nc.sync.dma_start(out=us_sb[:], in_=us.rearrange("(p t) o -> p (t o)", t=PACK))
-        load_scale_quadrants(nc.sync, wb_raw[:, 0:N], wb_scales[0], range(QUADS))
-        nc.sync.dma_start(out=wb_raw[:, N : 3 * N].bitcast(I32), in_=wb_words[0].bitcast(I32))
 
         sums = keep.tile([P, CHUNKS, PACK], F32, name="sums")
 
@@ -80,14 +81,19 @@ def tile_list_hidden_evened_pl_kernel(
         magnitudes = keep.tile([P, CHUNKS, PACK, CHUNK], BF16, name="magnitudes")
         for h in range(2):
             cols = offsets[:, h * HALF // 16 : (h + 1) * HALF // 16]
-            g_scales = keep.tile([P, HALF], U8, name=f"g_scales{h}", align_bytes=64)
-            g_words = keep.tile([P, HALF], U16, name=f"g_words{h}", align_bytes=64)
-            nc.vector.tensor_copy(out=g_words[:], in_=x_words[:].indirect(cols))
+            if h == 0:
+                g_scales = keep.tile([P, HALF], U8, name="g_scales0", align_bytes=64)
+                g_words = keep.tile([P, HALF], U16, name="g_words0", align_bytes=64)
+            else:
+                g_words = shared.tile([P, HALF], U16, name="g_words1", offset=64, align_bytes=64)
+                g_scales = shared.tile([P, HALF], U8, name="g_scales1", offset=64 + 2 * HALF, align_bytes=64)
             nc.vector.tensor_copy(out=g_scales[:], in_=x_scales[:].indirect(cols))
+            nc.vector.tensor_copy(out=g_words[:], in_=x_words[:].indirect(cols))
             if h == 0:
                 nc.vector.tensor_copy(
                     out=wa_codes[:].rearrange("p t m -> p m t"), in_=wa_raw[:].rearrange("p (m t) -> p m t", t=PACK)
                 )
+                nc.vector.tensor_copy(out=wa_scale[:], in_=wa_scale_raw[:].rearrange("p (m t) -> p t m", t=PACK))
             for u in range(2):
                 c = 2 * h + u
                 bank = psum.tile([P, PACK, CHUNK], F32, name=f"a_bank{c}")
@@ -104,14 +110,11 @@ def tile_list_hidden_evened_pl_kernel(
                     )
                 a_banks.append(bank)
 
-        rw_rows = keep.tile([P, J], F32, name="rw_rows", tag="wa_raw", align_bytes=64)
-        nc.sync.dma_start(out=rw_rows[:], in_=rw[0].partition_broadcast(P))
-
         wb_codes = keep.tile([P, PACK, P], U16, name="wb_codes", align_bytes=64)
         wb_scale = keep.tile([P, PACK, P], U8, name="wb_scale", align_bytes=64)
-        nc.vector.tensor_copy(out=wb_scale[:], in_=wb_raw[:, 0:N].rearrange("p (m t) -> p t m", t=PACK))
+        nc.vector.tensor_copy(out=wb_scale[:], in_=wb_scale_raw[:].rearrange("p (m t) -> p t m", t=PACK))
         nc.vector.tensor_copy(
-            out=wb_codes[:], in_=wb_raw[:, N : 3 * N].bitcast(U16).rearrange("p (m t) -> p t m", t=PACK)
+            out=wb_codes[:], in_=wb_raw[:].rearrange("p (m t) -> p t m", t=PACK)
         )
 
         inv_us = keep.tile([P, PACK], F32, name="inv_us")
@@ -205,7 +208,10 @@ def tile_list_hidden_evened_pl_kernel(
                 op=ALU.mult,
             )
             nc.sync.dma_start(out=y_rows[:, :, js], in_=y[c][:])
-            nc.scalar.copy(
+
+        def round_y(c):
+            copy = nc.vector.tensor_copy if c == CHUNKS - 1 else nc.scalar.copy
+            copy(
                 out=y16[c][:].rearrange("p (g i) t -> p g t i", i=4),
                 in_=y[c][:].rearrange("p t (g i) -> p g t i", i=4),
             )
@@ -216,25 +222,29 @@ def tile_list_hidden_evened_pl_kernel(
                 out=y_codes[:, js].bitcast(FP8X4), scales=y_scale[:, js], in_=y16[c][:].rearrange("p j t -> p (j t)")
             )
 
+        words_out = out_1[0].rearrange("p c t -> p (c t)").bitcast(I32)
         scale_hid(0)
-        scale_hid(1)
-        scale_hid_on_scalar(2)
+        scale_hid_on_scalar(1)
+        scale_hid(2)
         scale_hid_on_scalar(3)
         second_product(0)
         second_product(1)
         second_product(2)
         weigh(0)
-        weigh(1)
+        round_y(0)
         second_product(3)
+        weigh(1)
+        round_y(1)
         weigh(2)
+        round_y(2)
+        weigh(3)
         planes(0)
         planes(1)
-        weigh(3)
+        nc.sync.dma_start(out=words_out[:, 0:HALF], in_=y_codes[:, 0:HALF].bitcast(I32))
+        round_y(3)
         planes(2)
-        words_out = out_1[0].rearrange("p c t -> p (c t)").bitcast(I32)
-        nc.sync.dma_start(out=words_out[:, 0 : 3 * CHUNK], in_=y_codes[:, 0 : 3 * CHUNK].bitcast(I32))
         planes(3)
-        nc.sync.dma_start(out=words_out[:, 3 * CHUNK : J], in_=y_codes[:, 3 * CHUNK : J].bitcast(I32))
+        nc.sync.dma_start(out=words_out[:, HALF:J], in_=y_codes[:, HALF:J].bitcast(I32))
         for q in range(QUADS):
             queue = nc.scalar if q % 2 == 0 else nc.sync
             queue.dma_start(

from contextlib import ExitStack

import concourse.mybir as mybir

K, T, J, R, N = 512, 2048, 512, 512, 512
FLOPS = 2 * K * R * J + 2 * R * N * J

F32 = mybir.dt.float32
BF16 = mybir.dt.bfloat16
I32 = mybir.dt.int32
U32 = mybir.dt.uint32
U16 = mybir.dt.uint16
U8 = mybir.dt.uint8
FP8X4 = mybir.dt.float8_e4m3fn_x4
FP4X4 = mybir.dt.float4_e2m1fn_x4
ACT = mybir.ActivationFunctionType
ALU = mybir.AluOpType
AX = mybir.AxisListType

P = 128
PACK = 4
QUADS = 4
CHUNK = 128
CHUNKS = J // CHUNK
HALF = J // 2
VECTOR_SUM_CHUNK = 1


def load_scale_rows(queue, plane, rows, quads):
    for q in quads:
        queue.dma_start(out=plane[32 * q : 32 * q + 4, :].bitcast(I32), in_=rows[4 * q : 4 * q + 4, :].bitcast(I32))


def load_scale_quadrants(queue, plane, rows, quads):
    width = rows.shape[1] // 4
    for q in quads:
        four = rows[4 * q : 4 * q + 4, :].bitcast(I32)
        queue.dma_start(
            out=plane[32 * q : 32 * q + 32, :].bitcast(I32), in_=four.unsqueeze(0).to_broadcast([8, 4, width])
        )


def tile_list_hidden_evened_pl_kernel(
    tc, xt_words, xt_scales, wa_words, wa_scales, us, wb_words, wb_scales, rw, offs, out_0, out_1, out_2
):
    nc = tc.nc
    with ExitStack() as ctx:
        keep = ctx.enter_context(tc.tile_pool(name="keep", bufs=1))
        shared = ctx.enter_context(tc.tile_pool(name="shared", bufs=1))
        psum = ctx.enter_context(tc.psum_pool(name="psum", bufs=1))

        offsets = keep.tile([P, J // 16], U16, name="offsets")
        x_words = keep.tile([P, T], U16, name="x_words", align_bytes=64)
        x_scales = keep.tile([P, T], U8, name="x_scales", align_bytes=64)
        wa_raw = keep.tile([P, R], I32, name="wa_raw", align_bytes=64)
        wa_scale_raw = shared.tile([P, R], U8, name="wa_scale_raw", offset=2 * HALF, align_bytes=64)
        wb_raw = keep.tile([P, N], U16, name="wb_raw", align_bytes=64)
        wb_scale_raw = keep.tile([P, N], U8, name="wb_scale_raw", align_bytes=64)
        us_sb = keep.tile([P, PACK], F32, name="us_sb")
        rw_rows = keep.tile([P, J], F32, name="rw_rows")

        nc.vector.memset(x_scales[:].bitcast(I32), 0)

        nc.sync.dma_start(offsets[:], offs)
        load_scale_rows(nc.scalar, x_scales, xt_scales[0], range(QUADS))
        load_scale_quadrants(nc.sync, wa_scale_raw, wa_scales[0], (0,))
        nc.sync.dma_start(out=x_words[:].bitcast(I32), in_=xt_words[0].bitcast(I32))
        nc.sync.dma_start(out=wa_raw[:], in_=wa_words[0].rearrange("p c t -> p (c t)").bitcast(I32))
        load_scale_quadrants(nc.sync, wa_scale_raw, wa_scales[0], (1, 2, 3))
        nc.sync.dma_start(out=us_sb[:], in_=us.rearrange("(p t) o -> p (t o)", t=PACK))
        load_scale_quadrants(nc.sync, wb_scale_raw, wb_scales[0], range(QUADS))
        nc.sync.dma_start(out=wb_raw[:].bitcast(I32), in_=wb_words[0].bitcast(I32))
        nc.sync.dma_start(out=rw_rows[:], in_=rw[0].partition_broadcast(P))

        wa_codes = keep.tile([P, PACK, P], I32, name="wa_codes", align_bytes=64)
        wa_scale = keep.tile([P, PACK, P], U8, name="wa_scale", align_bytes=64)

        sums = keep.tile([P, CHUNKS, PACK], F32, name="sums")

        a_banks = []
        magnitudes = keep.tile([P, CHUNKS, PACK, CHUNK], BF16, name="magnitudes")
        for h in range(2):
            cols = offsets[:, h * HALF // 16 : (h + 1) * HALF // 16]
            if h == 0:
                g_scales = keep.tile([P, HALF], U8, name="g_scales0", align_bytes=64)
                g_words = keep.tile([P, HALF], U16, name="g_words0", align_bytes=64)
            else:
                g_words = shared.tile([P, HALF], U16, name="g_words1", offset=64, align_bytes=64)
                g_scales = shared.tile([P, HALF], U8, name="g_scales1", offset=64 + 2 * HALF, align_bytes=64)
            nc.vector.tensor_copy(out=g_scales[:], in_=x_scales[:].indirect(cols))
            nc.vector.tensor_copy(out=g_words[:], in_=x_words[:].indirect(cols))
            if h == 0:
                nc.vector.tensor_copy(
                    out=wa_codes[:].rearrange("p t m -> p m t"), in_=wa_raw[:].rearrange("p (m t) -> p m t", t=PACK)
                )
                nc.vector.tensor_copy(out=wa_scale[:], in_=wa_scale_raw[:].rearrange("p (m t) -> p t m", t=PACK))
            for u in range(2):
                c = 2 * h + u
                bank = psum.tile([P, PACK, CHUNK], F32, name=f"a_bank{c}")
                js = slice(u * CHUNK, (u + 1) * CHUNK)
                for t in range(PACK):
                    nc.tensor.matmul_mx(
                        out=bank[:, t, :],
                        lhsT=wa_codes[:, t, :].bitcast(FP8X4),
                        lhsT_scale=wa_scale[:, t, :],
                        rhs=g_words[:, js].bitcast(FP4X4),
                        rhs_scale=g_scales[:, js],
                        start=True,
                        stop=True,
                    )
                a_banks.append(bank)

        wb_codes = keep.tile([P, PACK, P], U16, name="wb_codes", align_bytes=64)
        wb_scale = keep.tile([P, PACK, P], U8, name="wb_scale", align_bytes=64)
        nc.vector.tensor_copy(out=wb_scale[:], in_=wb_scale_raw[:].rearrange("p (m t) -> p t m", t=PACK))
        nc.vector.tensor_copy(
            out=wb_codes[:], in_=wb_raw[:].rearrange("p (m t) -> p t m", t=PACK)
        )

        inv_us = keep.tile([P, PACK], F32, name="inv_us")
        nc.vector.reciprocal(out=inv_us[:], in_=us_sb[:])
        for c in range(CHUNKS):
            if c == VECTOR_SUM_CHUNK:
                a_copy = keep.tile([P, PACK, CHUNK], F32, name="a_copy")
                nc.vector.tensor_copy(out=a_copy[:], in_=a_banks[c][:])
                nc.vector.tensor_reduce(
                    out=sums[:, c, :], in_=a_copy[:], axis=AX.X, op=ALU.add, apply_absolute_value=True
                )
            else:
                for t in range(PACK):
                    nc.scalar.activation(
                        out=magnitudes[:, c, t, :], in_=a_banks[c][:, t, :], func=ACT.Abs, accum_out=sums[:, c, t : t + 1]
                    )

        early = keep.tile([P, PACK], F32, name="early")
        early2 = keep.tile([P, PACK], F32, name="early2")
        denom = keep.tile([P, PACK], F32, name="denom")
        factor = keep.tile([P, PACK], F32, name="factor")
        slope = keep.tile([P, PACK], F32, name="slope")
        nc.vector.tensor_scalar(out=slope[:], in0=inv_us[:], scalar1=1.0 / J, scalar2=None, op0=ALU.mult)
        nc.vector.scalar_tensor_tensor(
            out=early[:], in0=sums[:, 0, :], scalar=0.1 * J, in1=sums[:, 1, :], op0=ALU.add, op1=ALU.add
        )
        nc.vector.tensor_tensor(out=early2[:], in0=early[:], in1=sums[:, 2, :], op=ALU.add)
        for t in range(PACK):
            nc.vector.tensor_scalar(
                out=denom[:, t : t + 1],
                in0=sums[:, 3, t : t + 1],
                scalar1=early2[:, t : t + 1],
                scalar2=slope[:, t : t + 1],
                op0=ALU.add,
                op1=ALU.mult,
            )
        nc.vector.reciprocal(out=factor[:], in_=denom[:])

        hid = [keep.tile([P, CHUNK, PACK], BF16, name=f"hid{c}", align_bytes=64) for c in range(CHUNKS)]
        h_codes = [keep.tile([P, CHUNK], U32, name=f"h_codes{c}", align_bytes=64) for c in range(CHUNKS)]
        h_scale = [keep.tile([P, CHUNK], U8, name=f"h_scale{c}", align_bytes=64) for c in range(CHUNKS)]
        y = [keep.tile([P, PACK, CHUNK], F32, name=f"y{c}", align_bytes=64) for c in range(CHUNKS)]
        y16 = [keep.tile([P, CHUNK, PACK], BF16, name=f"y16_{c}", align_bytes=64) for c in range(CHUNKS)]
        y_codes = keep.tile([P, J], U32, name="y_codes", align_bytes=64)
        y_scale = keep.tile([P, J], U8, name="y_scale", align_bytes=64)
        p_banks = {}
        y_rows = out_0.rearrange("(p t) j -> p t j", t=PACK)

        def scale_hid(c):
            nc.vector.tensor_tensor(
                out=hid[c][:],
                in0=a_banks[c][:].rearrange("p t j -> p j t"),
                in1=factor[:].unsqueeze(1).to_broadcast([P, CHUNK, PACK]),
                op=ALU.mult,
            )

        def scale_hid_on_scalar(c):
            rows = keep.tile([P, PACK, CHUNK], BF16, name=f"hid_rows{c}")
            for t in range(PACK):
                nc.scalar.activation(
                    out=rows[:, t, :], in_=a_banks[c][:, t, :], func=ACT.Copy, scale=factor[:, t : t + 1]
                )
            nc.scalar.copy(
                out=hid[c][:].rearrange("p (g i) t -> p g t i", i=4),
                in_=rows[:].rearrange("p t (g i) -> p g t i", i=4),
            )

        def second_product(c):
            nc.vector.quantize_mx(
                out=h_codes[c][:].bitcast(FP8X4), scales=h_scale[c][:], in_=hid[c][:].rearrange("p j t -> p (j t)")
            )
            bank = psum.tile([P, PACK, CHUNK], F32, name=f"p_bank{c}", tag=f"p_bank{c}")
            for t in range(PACK):
                nc.tensor.matmul_mx(
                    out=bank[:, t, :],
                    lhsT=wb_codes[:, t, :].bitcast(FP4X4),
                    lhsT_scale=wb_scale[:, t, :],
                    rhs=h_codes[c][:].bitcast(FP8X4),
                    rhs_scale=h_scale[c][:],
                    start=True,
                    stop=True,
                )
            p_banks[c] = bank

        def weigh(c):
            js = slice(c * CHUNK, (c + 1) * CHUNK)
            nc.vector.tensor_tensor(
                out=y[c][:],
                in0=p_banks[c][:],
                in1=rw_rows[:, js].unsqueeze(1).to_broadcast([P, PACK, CHUNK]),
                op=ALU.mult,
            )
            nc.sync.dma_start(out=y_rows[:, :, js], in_=y[c][:])

        def round_y(c):
            copy = nc.vector.tensor_copy if c == CHUNKS - 1 else nc.scalar.copy
            copy(
                out=y16[c][:].rearrange("p (g i) t -> p g t i", i=4),
                in_=y[c][:].rearrange("p t (g i) -> p g t i", i=4),
            )

        def planes(c):
            js = slice(c * CHUNK, (c + 1) * CHUNK)
            nc.vector.quantize_mx(
                out=y_codes[:, js].bitcast(FP8X4), scales=y_scale[:, js], in_=y16[c][:].rearrange("p j t -> p (j t)")
            )

        words_out = out_1[0].rearrange("p c t -> p (c t)").bitcast(I32)
        scale_hid(0)
        scale_hid_on_scalar(1)
        scale_hid(2)
        scale_hid_on_scalar(3)
        second_product(0)
        second_product(1)
        second_product(2)
        weigh(0)
        round_y(0)
        second_product(3)
        weigh(1)
        round_y(1)
        weigh(2)
        round_y(2)
        weigh(3)
        planes(0)
        planes(1)
        nc.sync.dma_start(out=words_out[:, 0:HALF], in_=y_codes[:, 0:HALF].bitcast(I32))
        round_y(3)
        planes(2)
        planes(3)
        nc.sync.dma_start(out=words_out[:, HALF:J], in_=y_codes[:, HALF:J].bitcast(I32))
        for q in range(QUADS):
            queue = nc.scalar if q % 2 == 0 else nc.sync
            queue.dma_start(
                out=out_2[0, 4 * q : 4 * q + 4, :].bitcast(I32), in_=y_scale[32 * q : 32 * q + 4, :].bitcast(I32)
            )
